import numpy as np
import ml_dtypes


def mxq(x, axis, fmt="e4m3"):
    dtype, down = {"e4m3": (ml_dtypes.float8_e4m3fn, 7), "e5m2": (ml_dtypes.float8_e5m2, 14)}[fmt]
    v = np.moveaxis(np.asarray(x, np.float32).astype(ml_dtypes.bfloat16).astype(np.float64), axis, -1)
    blocks = v.reshape(v.shape[:-1] + (-1, 32))
    amax = np.abs(blocks).max(-1, keepdims=True)
    byte = np.maximum(np.where(amax > 0, np.frexp(amax)[1] - 1 + 127, 0) - down, 1)
    scale = np.exp2(byte - 127.0)
    codes = (blocks / scale).astype(np.float32).astype(dtype).astype(np.float64)
    return np.moveaxis((codes * scale).reshape(v.shape), -1, axis)


WIDE = False


def mx_kscale(k):
    if not WIDE:
        return np.ones(k)
    levels = np.array([10, -10, 5, -5, 0])
    if k % 512:
        return np.exp2(np.random.permutation(np.resize(levels, k // 32))).repeat(32)
    a = np.empty((k // 512, 16))
    for p in range(k // 512):
        a[p, :8] = np.random.permutation(np.resize(levels, 8))
        for g in range(8):
            far = levels[np.abs(levels - a[p, g]) >= 10]
            a[p, g + 8] = far[np.random.randint(len(far))]
    return np.exp2(a.ravel()).repeat(32)


def f64(x):
    return np.asarray(x).astype(np.float64)


def striped(idx):
    return np.tile(np.asarray(idx).reshape(-1, 16).T, (8, 1)).astype(np.uint16)


def unstriped(offs):
    return offs[:16].T.reshape(-1).astype(np.int64)


E2M1 = np.array([0.0, 0.5, 1.0, 1.5, 2.0, 3.0, 4.0, 6.0, -0.0, -0.5, -1.0, -1.5, -2.0, -3.0, -4.0, -6.0])


def pack_weight(w, fmt):
    k, n = w.shape
    w = f64(np.asarray(w, np.float32).astype(ml_dtypes.bfloat16)).reshape(k // 32, 32, n)
    amax = np.abs(w).max(1)
    if fmt == "e4m3":
        byte = np.frexp(amax)[1] - 1 + 127 - 7
    else:
        mant, ex = np.frexp(amax / 6.0)
        byte = np.where(mant > 0.5, ex, ex - 1) + 127
    byte = np.clip(np.where(amax > 0, byte, 1), 1, 254)
    scaled = (w * np.exp2(127.0 - byte)[:, None, :]).reshape(k, n).astype(np.float32)
    by_word = np.ascontiguousarray(scaled.reshape(k // 512, 128, 4, n).transpose(0, 1, 3, 2))
    if fmt == "e4m3":
        words = by_word.astype(ml_dtypes.float8_e4m3fn).view(np.uint8)
    else:
        c = by_word.astype(ml_dtypes.float4_e2m1fn).view(np.uint8) & 0xF
        words = (c[..., 0::2] | (c[..., 1::2] << 4)).reshape(k // 512, 128, 2 * n)
    return np.ascontiguousarray(words), np.ascontiguousarray(byte.astype(np.uint8).reshape(k // 512, 16, n))


def unpack_weight(words, scales, fmt):
    g, _, n = scales.shape
    words = np.ascontiguousarray(words).reshape(g, 128, n, -1)
    if fmt == "e4m3":
        vals = words.view(ml_dtypes.float8_e4m3fn).astype(np.float64)
    else:
        nib = np.empty((g, 128, n, 4), np.uint8)
        nib[..., 0::2] = words & 0xF
        nib[..., 1::2] = words >> 4
        vals = E2M1[nib]
    vals = vals * np.repeat(np.exp2(scales.astype(np.float64) - 127.0), 8, axis=1)[..., None]
    return vals.transpose(0, 1, 3, 2).reshape(g * 512, n)


D, E, T, I, Q = 512, 512, 2048, 512, 128


def setup_inputs():
    n = np.random.standard_normal
    idx = np.random.permutation(T)[:I]
    fd = mx_kscale(D)
    fe = mx_kscale(E)
    keysp = pack_weight(n((D, T)) / fd[:, None], "e2m1")
    valsp = pack_weight(n((E, T)) / fe[:, None], "e2m1")
    return {
        "query": (n((D, Q)) * 0.8 / np.sqrt(D) * fd[:, None]).astype(np.float32),
        "keys_words": keysp[0],
        "keys_scales": keysp[1],
        "averse": (np.random.uniform(0.4, 1.0, (Q, 1))).astype(np.float32),
        "gout": (n((E, Q)) * 1 / np.sqrt(E) * fe[:, None]).astype(np.float32),
        "vals_words": valsp[0],
        "vals_scales": valsp[1],
        "dquery": (n((D, Q)) * 1.0 / np.sqrt(D) * fd[:, None]).astype(np.float32),
        "base": (0.5 * n((Q, T))).astype(np.float32),
        "offs": striped(idx),
    }


def reference(query, keys_words, keys_scales, averse, gout, vals_words, vals_scales, dquery, base, offs):
    idx = unstriped(offs)
    keysu = unpack_weight(keys_words, keys_scales, "e2m1")
    valsu = unpack_weight(vals_words, vals_scales, "e2m1")
    queryq = mxq(f64(query), 0, "e4m3")
    keysidxg = keysu[:, idx]
    a = queryq.T @ keysidxg
    dqueryq = mxq(f64(dquery), 0, "e4m3")
    ta = dqueryq.T @ keysidxg
    p = np.exp(a - np.max(a, axis=1, keepdims=True))
    p2 = np.exp(a * (-1.0) - np.max(a * (-1.0), axis=1, keepdims=True))
    goutq = mxq(f64(gout), 0, "e4m3")
    valsidxg = valsu[:, idx]
    c0 = goutq.T @ valsidxg
    dr2 = c0 * (-1.0) * f64(averse)
    dp2 = dr2 / np.sum(p2, axis=1, keepdims=True) + np.sum(dr2 * p2 / np.square(np.sum(p2, axis=1, keepdims=True)) * (-1.0), axis=1, keepdims=True)
    dp = c0 / np.sum(p, axis=1, keepdims=True) + np.sum(c0 * p / np.square(np.sum(p, axis=1, keepdims=True)) * (-1.0), axis=1, keepdims=True)
    tp = ta * p
    tp2 = ta * (-1.0) * p2
    tdp2 = np.sum(tp2, axis=1, keepdims=True) * dr2 / np.square(np.sum(p2, axis=1, keepdims=True)) * (-1.0) + np.sum((tp2 * dr2 - np.sum(tp2, axis=1, keepdims=True) * np.sum(p2, axis=1, keepdims=True) * 2.0 * dr2 * p2 / np.square(np.sum(p2, axis=1, keepdims=True))) / np.square(np.sum(p2, axis=1, keepdims=True)) * (-1.0), axis=1, keepdims=True)
    tdp = np.sum(tp, axis=1, keepdims=True) * c0 / np.square(np.sum(p, axis=1, keepdims=True)) * (-1.0) + np.sum((tp * c0 - np.sum(tp, axis=1, keepdims=True) * np.sum(p, axis=1, keepdims=True) * 2.0 * c0 * p / np.square(np.sum(p, axis=1, keepdims=True))) / np.square(np.sum(p, axis=1, keepdims=True)) * (-1.0), axis=1, keepdims=True)
    tda = tdp * p + tp * dp - (tdp2 * p2 + tp2 * dp2)
    gs = tda * 512.0
    gf = np.zeros((Q, T))
    gf[:, idx] = gs
    y = f64(base) + gf
    return y

@@ -1,0 +1,167 @@
+from contextlib import ExitStack
+
+import concourse.mybir as mybir
+
+D, T, SLOTS, Q = 512, 2048, 512, 128
+FLOPS = 3 * 2 * D * Q * SLOTS
+
+F32 = mybir.dt.float32
+BF16 = mybir.dt.bfloat16
+I32 = mybir.dt.int32
+U32 = mybir.dt.uint32
+U16 = mybir.dt.uint16
+U8 = mybir.dt.uint8
+FP8X4 = mybir.dt.float8_e4m3fn_x4
+FP4X4 = mybir.dt.float4_e2m1fn_x4
+ALU = mybir.AluOpType
+ACT = mybir.ActivationFunctionType
+AXIS = mybir.AxisListType
+
+P = 128
+PACK = 4
+GAIN = 512.0
+STORE_COLS = 512
+
+
+def tile_attend_hvdirect_twoside_s_kernel(
+    tc, query, keys_words, keys_scales, averse, gout, vals_words, vals_scales, dquery, base, offs, out
+):
+    nc = tc.nc
+    with ExitStack() as ctx:
+        held = ctx.enter_context(tc.tile_pool(name="held", bufs=1))
+        psum = ctx.enter_context(tc.psum_pool(name="psum", bufs=1))
+
+        def sb(name, cols, dtype=F32):
+            return held.tile([P, cols], dtype, name=name, align_bytes=64)
+
+        offsets = held.tile([P, SLOTS // 16], U16, name="offsets")
+        nc.sync.dma_start(offsets[:], offs)
+
+        def load_scales(name, scales, queue, clear):
+            plane = sb(name, T, U8)
+            clear.memset(plane[:].bitcast(I32), 0)
+            for quad in range(4):
+                queue.dma_start(
+                    plane[32 * quad : 32 * quad + 4, :].bitcast(I32),
+                    scales[0, 4 * quad : 4 * quad + 4, :].bitcast(I32),
+                )
+            return plane
+
+        def load_words(name, words):
+            pool = sb(name, T, U16)
+            nc.sync.dma_start(pool[:].bitcast(I32), words[0].bitcast(I32))
+            return pool
+
+        def load_rows(name, rows):
+            raw = held.tile([P, PACK, Q], F32, name=name, align_bytes=64)
+            nc.sync.dma_start(raw[:], rows.rearrange("(p j) q -> p j q", j=PACK))
+            return raw
+
+        key_plane = load_scales("key_plane", keys_scales, nc.scalar, nc.vector)
+        key_pool = load_words("key_pool", keys_words)
+        query_raw = load_rows("query_raw", query)
+        dquery_raw = load_rows("dquery_raw", dquery)
+        val_plane = load_scales("val_plane", vals_scales, nc.sync, nc.gpsimd)
+        val_pool = load_words("val_pool", vals_words)
+        gout_raw = load_rows("gout_raw", gout)
+        av = sb("av", 1)
+        nc.sync.dma_start(av[:], averse)
+        result = sb("result", T)
+        nc.sync.dma_start(result[:], base)
+
+        placed = sb("placed", T)
+        nc.vector.memset(placed[:], 0.0)
+
+        def gather(name, window, dtype):
+            picked = sb(name, SLOTS, dtype)
+            nc.vector.tensor_copy(picked[:], window[:].indirect(offsets[:]))
+            return picked
+
+        def quantize(name, raws):
+            cols = Q * len(raws)
+            grouped = held.tile([P, cols, PACK], BF16, name=name + "_bf16", align_bytes=64)
+            for n, raw in enumerate(raws):
+                nc.scalar.copy(
+                    grouped[:, n * Q : (n + 1) * Q, :].rearrange("p (c i) t -> p c t i", i=4),
+                    raw[:].rearrange("p t (c i) -> p c t i", i=4),
+                )
+            codes = sb(name + "_codes", cols, U32)
+            plane = sb(name + "_plane", cols, U8)
+            nc.vector.quantize_mx(
+                out=codes[:].bitcast(FP8X4), scales=plane[:], in_=grouped[:].rearrange("p c t -> p (c t)")
+            )
+            return codes, plane
+
+        def product(name, codes, plane, n, words, scales):
+            acc = psum.tile([Q, SLOTS], F32, name=name)
+            cols = slice(n * Q, (n + 1) * Q)
+            nc.tensor.matmul_mx(
+                out=acc[:],
+                lhsT=codes[:, cols].bitcast(FP8X4),
+                lhsT_scale=plane[:, cols],
+                rhs=words[:].bitcast(FP4X4),
+                rhs_scale=scales[:],
+                start=True,
+                stop=True,
+            )
+            return acc
+
+        key_scales = gather("key_scales", key_plane, U8)
+        key_words = gather("key_words", key_pool, U16)
+        q_codes, q_plane = quantize("q", [query_raw, dquery_raw])
+        a = product("a", q_codes, q_plane, 0, key_words, key_scales)
+        ta = product("ta", q_codes, q_plane, 1, key_words, key_scales)
+
+        val_words = gather("val_words", val_pool, U16)
+
+        neg_a = sb("neg_a", SLOTS)
+        neg_max = sb("neg_max", 1)
+        nc.vector.tensor_scalar(neg_a[:], a[:], -1.0, None, ALU.mult, ALU.min, accum_out=neg_max[:])
+        p1, sum1 = sb("p1", SLOTS), sb("sum1", 1)
+        nc.scalar.activation(p1[:], a[:], ACT.Exp, bias=neg_max[:], scale=1.0, accum_out=sum1[:])
+
+        val_scales = gather("val_scales", val_plane, U8)
+
+        low = sb("low", 1)
+        nc.vector.tensor_reduce(low[:], neg_a[:], AXIS.X, ALU.max, negate=True)
+        p2, sum2 = sb("p2", SLOTS), sb("sum2", 1)
+        nc.scalar.activation(p2[:], neg_a[:], ACT.Exp, bias=low[:], scale=1.0, accum_out=sum2[:])
+
+        g_codes, g_plane = quantize("g", [gout_raw])
+        c0 = product("c0", g_codes, g_plane, 0, val_words, val_scales)
+
+        sides = (0, 1)
+        p = (p1, p2)
+        total = (sum1, sum2)
+
+        def pair(name, cols):
+            return [sb(name + str(s), cols) for s in sides]
+
+        inv, gain, mean_t, sum_c, cross, centre, lift = (
+            pair(name, 1) for name in ("inv", "gain", "mean_t", "sum_c", "cross", "centre", "lift")
+        )
+        pt, pc, pw, part, side = (pair(name, SLOTS) for name in ("pt", "pc", "pw", "part", "side"))
+
+        stt = nc.vector.scalar_tensor_tensor
+        for s in sides:
+            nc.vector.reciprocal(inv[s][:], total[s][:])
+            stt(pt[s][:], ta[:], inv[s][:], p[s][:], ALU.mult, ALU.mult, accum_out=mean_t[s][:])
+        nc.gpsimd.tensor_scalar(gain[0][:], inv[0][:], GAIN, 1.0, ALU.mult, ALU.mult)
+        nc.gpsimd.tensor_scalar(gain[1][:], inv[1][:], av[:], -GAIN, ALU.mult, ALU.mult)
+        for s in sides:
+            stt(pc[s][:], c0[:], gain[s][:], p[s][:], ALU.mult, ALU.mult, accum_out=sum_c[s][:])
+            nc.gpsimd.tensor_tensor(centre[s][:], sum_c[s][:], mean_t[s][:], ALU.mult)
+        for s in sides:
+            stt(pw[s][:], ta[:], mean_t[s][:], pc[s][:], ALU.subtract, ALU.mult, accum_out=cross[s][:])
+            nc.gpsimd.tensor_scalar(lift[s][:], centre[s][:], cross[s][:], inv[s][:], ALU.subtract, ALU.mult)
+        for s in sides:
+            stt(part[s][:], pt[s][:], sum_c[s][:], pw[s][:], ALU.mult, ALU.subtract)
+        for s in sides:
+            stt(side[s][:], p[s][:], lift[s][:], part[s][:], ALU.mult, ALU.subtract)
+
+        nc.vector.tensor_tensor(placed[:].indirect(offsets[:]), side[0][:], side[1][:], ALU.add)
+
+        for n, c in enumerate(range(0, T, STORE_COLS)):
+            cols = slice(c, c + STORE_COLS)
+            nc.vector.tensor_tensor(result[:, cols], result[:, cols], placed[:, cols], ALU.add)
+            (nc.sync, nc.scalar)[n % 2].dma_start(out[:, cols], result[:, cols])

@@ -31,8 +31,8 @@ def tile_attend_hvdirect_twoside_s_kernel(
         held = ctx.enter_context(tc.tile_pool(name="held", bufs=1))
         psum = ctx.enter_context(tc.psum_pool(name="psum", bufs=1))
 
-        def sb(name, cols, dtype=F32):
-            return held.tile([P, cols], dtype, name=name, align_bytes=64)
+        def sb(name, cols, dtype=F32, reuses=None):
+            return held.tile([P, cols], dtype, name=name, tag=reuses or name, align_bytes=64)
 
         offsets = held.tile([P, SLOTS // 16], U16, name="offsets")
         nc.sync.dma_start(offsets[:], offs)
@@ -40,11 +40,8 @@ def tile_attend_hvdirect_twoside_s_kernel(
         def load_scales(name, scales, queue, clear):
             plane = sb(name, T, U8)
             clear.memset(plane[:].bitcast(I32), 0)
-            for quad in range(4):
-                queue.dma_start(
-                    plane[32 * quad : 32 * quad + 4, :].bitcast(I32),
-                    scales[0, 4 * quad : 4 * quad + 4, :].bitcast(I32),
-                )
+            for row in range(4):
+                queue.dma_start(plane[row:P:32, :].bitcast(I32), scales[0, row:16:4, :].bitcast(I32))
             return plane
 
         def load_words(name, words):
@@ -57,29 +54,24 @@ def tile_attend_hvdirect_twoside_s_kernel(
             nc.sync.dma_start(raw[:], rows.rearrange("(p j) q -> p j q", j=PACK))
             return raw
 
-        key_plane = load_scales("key_plane", keys_scales, nc.scalar, nc.vector)
         key_pool = load_words("key_pool", keys_words)
+        key_plane = load_scales("key_plane", keys_scales, nc.sync, nc.vector)
         query_raw = load_rows("query_raw", query)
-        dquery_raw = load_rows("dquery_raw", dquery)
-        val_plane = load_scales("val_plane", vals_scales, nc.sync, nc.gpsimd)
         val_pool = load_words("val_pool", vals_words)
+        dquery_raw = load_rows("dquery_raw", dquery)
         gout_raw = load_rows("gout_raw", gout)
+        val_plane = load_scales("val_plane", vals_scales, nc.sync, nc.vector)
         av = sb("av", 1)
         nc.sync.dma_start(av[:], averse)
-        result = sb("result", T)
-        nc.sync.dma_start(result[:], base)
 
-        placed = sb("placed", T)
-        nc.vector.memset(placed[:], 0.0)
-
-        def gather(name, window, dtype):
-            picked = sb(name, SLOTS, dtype)
+        def gather(name, window, dtype, reuses=None):
+            picked = sb(name, SLOTS, dtype, reuses)
             nc.vector.tensor_copy(picked[:], window[:].indirect(offsets[:]))
             return picked
 
         def quantize(name, raws):
             cols = Q * len(raws)
-            grouped = held.tile([P, cols, PACK], BF16, name=name + "_bf16", align_bytes=64)
+            grouped = held.tile([P, cols, PACK], BF16, name=name + "_bf16", tag=name + "_bf16", align_bytes=64)
             for n, raw in enumerate(raws):
                 nc.scalar.copy(
                     grouped[:, n * Q : (n + 1) * Q, :].rearrange("p (c i) t -> p c t i", i=4),
@@ -106,29 +98,34 @@ def tile_attend_hvdirect_twoside_s_kernel(
             )
             return acc
 
-        key_scales = gather("key_scales", key_plane, U8)
         key_words = gather("key_words", key_pool, U16)
-        q_codes, q_plane = quantize("q", [query_raw, dquery_raw])
+        key_scales = gather("key_scales", key_plane, U8)
+        q_codes, q_plane = quantize("q", [query_raw])
         a = product("a", q_codes, q_plane, 0, key_words, key_scales)
-        ta = product("ta", q_codes, q_plane, 1, key_words, key_scales)
+        val_words = gather("val_words", val_pool, U16, reuses="q_bf16")
 
-        val_words = gather("val_words", val_pool, U16)
-
-        neg_a = sb("neg_a", SLOTS)
+        neg_a = sb("neg_a", SLOTS, reuses="val_pool")
         neg_max = sb("neg_max", 1)
         nc.vector.tensor_scalar(neg_a[:], a[:], -1.0, None, ALU.mult, ALU.min, accum_out=neg_max[:])
-        p1, sum1 = sb("p1", SLOTS), sb("sum1", 1)
-        nc.scalar.activation(p1[:], a[:], ACT.Exp, bias=neg_max[:], scale=1.0, accum_out=sum1[:])
-
-        val_scales = gather("val_scales", val_plane, U8)
-
         low = sb("low", 1)
-        nc.vector.tensor_reduce(low[:], neg_a[:], AXIS.X, ALU.max, negate=True)
+        nc.vector.tensor_reduce(low[:], a[:], AXIS.X, ALU.min)
+
+        g_codes, g_plane = quantize("g", [dquery_raw, gout_raw])
+        ta = product("ta", g_codes, g_plane, 0, key_words, key_scales)
+        val_scales = gather("val_scales", val_plane, U8)
+        c0 = product("c0", g_codes, g_plane, 1, val_words, val_scales)
+
+        p1, sum1 = sb("p1", SLOTS), sb("sum1", 1)
+        nc.scalar.activation(p1[:], neg_a[:], ACT.Exp, bias=neg_max[:], scale=-1.0, accum_out=sum1[:])
         p2, sum2 = sb("p2", SLOTS), sb("sum2", 1)
         nc.scalar.activation(p2[:], neg_a[:], ACT.Exp, bias=low[:], scale=1.0, accum_out=sum2[:])
+        ta_sb = sb("ta_sb", SLOTS)
+        nc.scalar.copy(ta_sb[:], ta[:])
 
-        g_codes, g_plane = quantize("g", [gout_raw])
-        c0 = product("c0", g_codes, g_plane, 0, val_words, val_scales)
+        result = []
+        for n, freed in enumerate(("key_pool", "val_pool")):
+            result.append(sb("result" + str(n), T // 2, reuses=freed))
+            nc.sync.dma_start(result[n][:], base[:, n * T // 2 : (n + 1) * T // 2])
 
         sides = (0, 1)
         p = (p1, p2)
@@ -137,31 +134,54 @@ def tile_attend_hvdirect_twoside_s_kernel(
         def pair(name, cols):
             return [sb(name + str(s), cols) for s in sides]
 
-        inv, gain, mean_t, sum_c, cross, centre, lift = (
-            pair(name, 1) for name in ("inv", "gain", "mean_t", "sum_c", "cross", "centre", "lift")
+        neg_inv, mean_t, mean_c, mean_c_inv, cross, centre, lift = (
+            pair(name, 1) for name in ("neg_inv", "mean_t", "mean_c", "mean_c_inv", "cross", "centre", "lift")
         )
-        pt, pc, pw, part, side = (pair(name, SLOTS) for name in ("pt", "pc", "pw", "part", "side"))
+        late = sb("late", SLOTS + 16, reuses="val_plane")
+        inv = (late[:, SLOTS : SLOTS + 1], late[:, SLOTS + 8 : SLOTS + 9])
+        rt = (sb("rt0", SLOTS), late[:, :SLOTS])
+        rc, pw = pair("rc", SLOTS), pair("pw", SLOTS)
+
+        def times(dst, src, factor, accum_out=None):
+            nc.scalar.activation(dst[:], src[:], ACT.Copy, scale=factor, accum_out=accum_out)
 
         stt = nc.vector.scalar_tensor_tensor
-        for s in sides:
+        for s in reversed(sides):
             nc.vector.reciprocal(inv[s][:], total[s][:])
-            stt(pt[s][:], ta[:], inv[s][:], p[s][:], ALU.mult, ALU.mult, accum_out=mean_t[s][:])
-        nc.gpsimd.tensor_scalar(gain[0][:], inv[0][:], GAIN, 1.0, ALU.mult, ALU.mult)
-        nc.gpsimd.tensor_scalar(gain[1][:], inv[1][:], av[:], -GAIN, ALU.mult, ALU.mult)
+            times(neg_inv[s], inv[s], -1.0)
+        pt = sb("pt", SLOTS)
+        nc.gpsimd.tensor_tensor(pt[:], p[0][:], ta_sb[:], ALU.mult)
+        placed = sb("placed", T, reuses="ta_sb")
+        nc.gpsimd.memset(placed[:], 0.0)
+        times(rt[0], pt, inv[0][:], accum_out=mean_t[0][:])
+        stt(rt[1][:], ta[:], inv[1][:], p[1][:], ALU.mult, ALU.mult, accum_out=mean_t[1][:])
         for s in sides:
-            stt(pc[s][:], c0[:], gain[s][:], p[s][:], ALU.mult, ALU.mult, accum_out=sum_c[s][:])
-            nc.gpsimd.tensor_tensor(centre[s][:], sum_c[s][:], mean_t[s][:], ALU.mult)
-        for s in sides:
-            stt(pw[s][:], ta[:], mean_t[s][:], pc[s][:], ALU.subtract, ALU.mult, accum_out=cross[s][:])
-            nc.gpsimd.tensor_scalar(lift[s][:], centre[s][:], cross[s][:], inv[s][:], ALU.subtract, ALU.mult)
-        for s in sides:
-            stt(part[s][:], pt[s][:], sum_c[s][:], pw[s][:], ALU.mult, ALU.subtract)
-        for s in sides:
-            stt(side[s][:], p[s][:], lift[s][:], part[s][:], ALU.mult, ALU.subtract)
+            stt(rc[s][:], c0[:], inv[s][:], p[s][:], ALU.mult, ALU.mult, accum_out=mean_c[s][:])
+            times(mean_c_inv[s], mean_c[s], inv[s][:])
+            times(centre[s], mean_t[s], mean_c_inv[s][:])
+        for s in reversed(sides):
+            stt(pw[s][:], ta[:], mean_t[s][:], rc[s][:], ALU.subtract, ALU.mult, accum_out=cross[s][:])
+            nc.scalar.activation(lift[s][:], cross[s][:], ACT.Identity, bias=centre[s][:], scale=neg_inv[s][:])
 
-        nc.vector.tensor_tensor(placed[:].indirect(offsets[:]), side[0][:], side[1][:], ALU.add)
+        half = SLOTS // 2
+        for h in range(2):
+            cols = slice(h * half, (h + 1) * half)
+            listed = placed[:].indirect(offsets[:, h * half // 16 : (h + 1) * half // 16])
+            if h == 0:
+                part, side = pair("part", half), pair("side", half)
+            else:
+                part = (sb("part_b0", half, reuses="side0"), sb("part_b1", half, reuses="side1"))
+                side = pair("side_b", half)
+            both = sb("both" + str(h), half)
+            for s in reversed(sides):
+                stt(part[s][:], rt[s][:, cols], mean_c[s][:], pw[s][:, cols], ALU.mult, ALU.subtract)
+            for s in reversed(sides):
+                stt(side[s][:], p[s][:, cols], lift[s][:], part[s][:], ALU.mult, ALU.subtract)
+            stt(both[:], side[1][:], av[:], side[0][:], ALU.mult, ALU.subtract)
+            nc.scalar.activation(listed, both[:], ACT.Copy, scale=-GAIN)
 
         for n, c in enumerate(range(0, T, STORE_COLS)):
             cols = slice(c, c + STORE_COLS)
-            nc.vector.tensor_tensor(result[:, cols], result[:, cols], placed[:, cols], ALU.add)
-            (nc.sync, nc.scalar)[n % 2].dma_start(out[:, cols], result[:, cols])
+            piece = result[c // (T // 2)][:, c % (T // 2) : c % (T // 2) + STORE_COLS]
+            nc.vector.tensor_tensor(piece, piece, placed[:, cols], ALU.add)
+            (nc.sync, nc.scalar)[n % 2].dma_start(out[:, cols], piece)

@@ -19,7 +19,11 @@ AXIS = mybir.AxisListType
 
 P = 128
 PACK = 4
+QUADRANT = 32
+LIST_ROWS = 16
 GAIN = 512.0
+HALF = SLOTS // 2
+BASE_COLS = T // 2
 STORE_COLS = 512
 
 
@@ -34,154 +38,143 @@ def tile_attend_hvdirect_twoside_s_kernel(
         def sb(name, cols, dtype=F32, reuses=None):
             return held.tile([P, cols], dtype, name=name, tag=reuses or name, align_bytes=64)
 
-        offsets = held.tile([P, SLOTS // 16], U16, name="offsets")
-        nc.sync.dma_start(offsets[:], offs)
+        def pair(name, cols):
+            return [sb(name + str(s), cols) for s in (0, 1)]
 
-        def load_scales(name, scales, queue, clear):
-            plane = sb(name, T, U8)
-            clear.memset(plane[:].bitcast(I32), 0)
-            for row in range(4):
-                queue.dma_start(plane[row:P:32, :].bitcast(I32), scales[0, row:16:4, :].bitcast(I32))
-            return plane
 
         def load_words(name, words):
             pool = sb(name, T, U16)
             nc.sync.dma_start(pool[:].bitcast(I32), words[0].bitcast(I32))
             return pool
 
+        def load_plane(name, scales):
+            plane = sb(name, T, U8)
+            nc.vector.memset(plane[:].bitcast(I32), 0)
+            for r in range(4):
+                nc.sync.dma_start(plane[r:P:QUADRANT, :].bitcast(I32), scales[0, r:16:4, :].bitcast(I32))
+            return plane
+
         def load_rows(name, rows):
-            raw = held.tile([P, PACK, Q], F32, name=name, align_bytes=64)
+            raw = held.tile([P, PACK, Q], F32, name=name, tag=name, align_bytes=64)
             nc.sync.dma_start(raw[:], rows.rearrange("(p j) q -> p j q", j=PACK))
             return raw
 
+        offsets = held.tile([P, SLOTS // LIST_ROWS], U16, name="offsets")
         key_pool = load_words("key_pool", keys_words)
-        key_plane = load_scales("key_plane", keys_scales, nc.sync, nc.vector)
+        nc.sync.dma_start(offsets[:], offs)
+        key_pool_plane = load_plane("key_pool_plane", keys_scales)
         query_raw = load_rows("query_raw", query)
         val_pool = load_words("val_pool", vals_words)
         dquery_raw = load_rows("dquery_raw", dquery)
         gout_raw = load_rows("gout_raw", gout)
-        val_plane = load_scales("val_plane", vals_scales, nc.sync, nc.vector)
+        val_pool_plane = load_plane("val_pool_plane", vals_scales)
         av = sb("av", 1)
         nc.sync.dma_start(av[:], averse)
+
 
         def gather(name, window, dtype, reuses=None):
             picked = sb(name, SLOTS, dtype, reuses)
             nc.vector.tensor_copy(picked[:], window[:].indirect(offsets[:]))
             return picked
 
-        def quantize(name, raws):
-            cols = Q * len(raws)
-            grouped = held.tile([P, cols, PACK], BF16, name=name + "_bf16", tag=name + "_bf16", align_bytes=64)
-            for n, raw in enumerate(raws):
-                nc.scalar.copy(
-                    grouped[:, n * Q : (n + 1) * Q, :].rearrange("p (c i) t -> p c t i", i=4),
-                    raw[:].rearrange("p t (c i) -> p c t i", i=4),
-                )
-            codes = sb(name + "_codes", cols, U32)
-            plane = sb(name + "_plane", cols, U8)
-            nc.vector.quantize_mx(
-                out=codes[:].bitcast(FP8X4), scales=plane[:], in_=grouped[:].rearrange("p c t -> p (c t)")
+        def quantize(name, raw):
+            grouped = held.tile([P, Q, PACK], BF16, name=name + "_bf16", tag=name + "_bf16", align_bytes=64)
+            nc.scalar.copy(
+                grouped[:].rearrange("p (c i) j -> p c j i", i=4), raw[:].rearrange("p j (c i) -> p c j i", i=4)
             )
-            return codes, plane
+            words = sb(name + "_words", Q, U32)
+            plane = sb(name + "_plane", Q, U8)
+            nc.vector.quantize_mx(
+                out=words[:].bitcast(FP8X4), scales=plane[:], in_=grouped[:].rearrange("p q j -> p (q j)")
+            )
+            return words, plane
 
-        def product(name, codes, plane, n, words, scales):
+        def product(name, rows, listed_words, listed_plane):
             acc = psum.tile([Q, SLOTS], F32, name=name)
-            cols = slice(n * Q, (n + 1) * Q)
             nc.tensor.matmul_mx(
                 out=acc[:],
-                lhsT=codes[:, cols].bitcast(FP8X4),
-                lhsT_scale=plane[:, cols],
-                rhs=words[:].bitcast(FP4X4),
-                rhs_scale=scales[:],
+                lhsT=rows[0][:].bitcast(FP8X4),
+                lhsT_scale=rows[1][:],
+                rhs=listed_words[:].bitcast(FP4X4),
+                rhs_scale=listed_plane[:],
                 start=True,
                 stop=True,
             )
             return acc
 
         key_words = gather("key_words", key_pool, U16)
-        key_scales = gather("key_scales", key_plane, U8)
-        q_codes, q_plane = quantize("q", [query_raw])
-        a = product("a", q_codes, q_plane, 0, key_words, key_scales)
-        val_words = gather("val_words", val_pool, U16, reuses="q_bf16")
+        key_plane = gather("key_plane", key_pool_plane, U8)
+        a = product("a", quantize("query", query_raw), key_words, key_plane)
+        val_words = gather("val_words", val_pool, U16, reuses="query_bf16")
+        ta = product("ta", quantize("dquery", dquery_raw), key_words, key_plane)
 
-        neg_a = sb("neg_a", SLOTS, reuses="val_pool")
-        neg_max = sb("neg_max", 1)
+        neg_a, neg_max, low = sb("neg_a", SLOTS), sb("neg_max", 1), sb("low", 1)
         nc.vector.tensor_scalar(neg_a[:], a[:], -1.0, None, ALU.mult, ALU.min, accum_out=neg_max[:])
-        low = sb("low", 1)
         nc.vector.tensor_reduce(low[:], a[:], AXIS.X, ALU.min)
 
-        g_codes, g_plane = quantize("g", [dquery_raw, gout_raw])
-        ta = product("ta", g_codes, g_plane, 0, key_words, key_scales)
-        val_scales = gather("val_scales", val_plane, U8)
-        c0 = product("c0", g_codes, g_plane, 1, val_words, val_scales)
+        gout_mx = quantize("gout", gout_raw)
+        val_plane = gather("val_plane", val_pool_plane, U8)
+        c0 = product("c0", gout_mx, val_words, val_plane)
 
-        p1, sum1 = sb("p1", SLOTS), sb("sum1", 1)
-        nc.scalar.activation(p1[:], neg_a[:], ACT.Exp, bias=neg_max[:], scale=-1.0, accum_out=sum1[:])
-        p2, sum2 = sb("p2", SLOTS), sb("sum2", 1)
-        nc.scalar.activation(p2[:], neg_a[:], ACT.Exp, bias=low[:], scale=1.0, accum_out=sum2[:])
-        ta_sb = sb("ta_sb", SLOTS)
+        p = (sb("p0", SLOTS, reuses="gout_raw"), sb("p1", SLOTS))
+        total = pair("total", 1)
+        nc.scalar.activation(p[0][:], neg_a[:], ACT.Exp, bias=neg_max[:], scale=-1.0, accum_out=total[0][:])
+        ta_sb = sb("ta_sb", SLOTS, reuses="neg_max")
         nc.scalar.copy(ta_sb[:], ta[:])
+        nc.scalar.activation(p[1][:], neg_a[:], ACT.Exp, bias=low[:], scale=1.0, accum_out=total[1][:])
 
         result = []
         for n, freed in enumerate(("key_pool", "val_pool")):
-            result.append(sb("result" + str(n), T // 2, reuses=freed))
-            nc.sync.dma_start(result[n][:], base[:, n * T // 2 : (n + 1) * T // 2])
+            result.append(sb("result" + str(n), BASE_COLS, reuses=freed))
+            nc.sync.dma_start(result[n][:], base[:, n * BASE_COLS : (n + 1) * BASE_COLS])
 
-        sides = (0, 1)
-        p = (p1, p2)
-        total = (sum1, sum2)
-
-        def pair(name, cols):
-            return [sb(name + str(s), cols) for s in sides]
-
-        neg_inv, mean_t, mean_c, mean_c_inv, cross, centre, lift = (
-            pair(name, 1) for name in ("neg_inv", "mean_t", "mean_c", "mean_c_inv", "cross", "centre", "lift")
+        neg_inv, mean_t, mean_c, mean_c_inv, means_inv, cov, p_factor = (
+            pair(name, 1) for name in ("neg_inv", "mean_t", "mean_c", "mean_c_inv", "means_inv", "cov", "p_factor")
         )
-        late = sb("late", SLOTS + 16, reuses="val_plane")
-        inv = (late[:, SLOTS : SLOTS + 1], late[:, SLOTS + 8 : SLOTS + 9])
-        rt = (sb("rt0", SLOTS), late[:, :SLOTS])
-        rc, pw = pair("rc", SLOTS), pair("pw", SLOTS)
+        rt = (sb("rt0", SLOTS), sb("rt1", SLOTS, reuses="val_pool_plane"))
+        rc, centred = pair("rc", SLOTS), pair("centred", SLOTS)
 
         def times(dst, src, factor, accum_out=None):
             nc.scalar.activation(dst[:], src[:], ACT.Copy, scale=factor, accum_out=accum_out)
 
         stt = nc.vector.scalar_tensor_tensor
-        for s in reversed(sides):
+
+        inv = {}
+        for s, freed in ((1, None), (0, "total1")):
+            inv[s] = sb("inv" + str(s), 1, reuses=freed)
             nc.vector.reciprocal(inv[s][:], total[s][:])
             times(neg_inv[s], inv[s], -1.0)
+
         pt = sb("pt", SLOTS)
         nc.gpsimd.tensor_tensor(pt[:], p[0][:], ta_sb[:], ALU.mult)
-        placed = sb("placed", T, reuses="ta_sb")
+        placed = sb("placed", T, reuses="neg_max")
         nc.gpsimd.memset(placed[:], 0.0)
         times(rt[0], pt, inv[0][:], accum_out=mean_t[0][:])
         stt(rt[1][:], ta[:], inv[1][:], p[1][:], ALU.mult, ALU.mult, accum_out=mean_t[1][:])
-        for s in sides:
+
+        for s in (0, 1):
             stt(rc[s][:], c0[:], inv[s][:], p[s][:], ALU.mult, ALU.mult, accum_out=mean_c[s][:])
             times(mean_c_inv[s], mean_c[s], inv[s][:])
-            times(centre[s], mean_t[s], mean_c_inv[s][:])
-        for s in reversed(sides):
-            stt(pw[s][:], ta[:], mean_t[s][:], rc[s][:], ALU.subtract, ALU.mult, accum_out=cross[s][:])
-            nc.scalar.activation(lift[s][:], cross[s][:], ACT.Identity, bias=centre[s][:], scale=neg_inv[s][:])
+            times(means_inv[s], mean_t[s], mean_c_inv[s][:])
+        for s in (1, 0):
+            stt(centred[s][:], ta[:], mean_t[s][:], rc[s][:], ALU.subtract, ALU.mult, accum_out=cov[s][:])
+            nc.scalar.activation(p_factor[s][:], cov[s][:], ACT.Identity, bias=means_inv[s][:], scale=neg_inv[s][:])
 
-        half = SLOTS // 2
-        for h in range(2):
-            cols = slice(h * half, (h + 1) * half)
-            listed = placed[:].indirect(offsets[:, h * half // 16 : (h + 1) * half // 16])
-            if h == 0:
-                part, side = pair("part", half), pair("side", half)
-            else:
-                part = (sb("part_b0", half, reuses="side0"), sb("part_b1", half, reuses="side1"))
-                side = pair("side_b", half)
-            both = sb("both" + str(h), half)
-            for s in reversed(sides):
-                stt(part[s][:], rt[s][:, cols], mean_c[s][:], pw[s][:, cols], ALU.mult, ALU.subtract)
-            for s in reversed(sides):
-                stt(side[s][:], p[s][:, cols], lift[s][:], part[s][:], ALU.mult, ALU.subtract)
-            stt(both[:], side[1][:], av[:], side[0][:], ALU.mult, ALU.subtract)
-            nc.scalar.activation(listed, both[:], ACT.Copy, scale=-GAIN)
+        for h in range(SLOTS // HALF):
+            cols = slice(h * HALF, (h + 1) * HALF)
+            entries = offsets[:, h * HALF // LIST_ROWS : (h + 1) * HALF // LIST_ROWS]
+            part = [sb("part%d%d" % (h, s), HALF, reuses="side0%d" % s if h else None) for s in (0, 1)]
+            side = pair("side%d" % h, HALF)
+            neg_tda = sb("neg_tda%d" % h, HALF)
+            for s in (1, 0):
+                stt(part[s][:], rt[s][:, cols], mean_c[s][:], centred[s][:, cols], ALU.mult, ALU.subtract)
+            for s in (1, 0):
+                stt(side[s][:], p[s][:, cols], p_factor[s][:], part[s][:], ALU.mult, ALU.subtract)
+            stt(neg_tda[:], side[1][:], av[:], side[0][:], ALU.mult, ALU.subtract)
+            nc.scalar.activation(placed[:].indirect(entries), neg_tda[:], ACT.Copy, scale=-GAIN)
 
-        for n, c in enumerate(range(0, T, STORE_COLS)):
-            cols = slice(c, c + STORE_COLS)
-            piece = result[c // (T // 2)][:, c % (T // 2) : c % (T // 2) + STORE_COLS]
+        for n, first in enumerate(range(0, T, STORE_COLS)):
+            cols = slice(first, first + STORE_COLS)
+            piece = result[first // BASE_COLS][:, first % BASE_COLS : first % BASE_COLS + STORE_COLS]
             nc.vector.tensor_tensor(piece, piece, placed[:, cols], ALU.add)
             (nc.sync, nc.scalar)[n % 2].dma_start(out[:, cols], piece)

from contextlib import ExitStack

import concourse.mybir as mybir

D, T, SLOTS, Q = 512, 2048, 512, 128
FLOPS = 3 * 2 * D * Q * SLOTS

F32 = mybir.dt.float32
BF16 = mybir.dt.bfloat16
I32 = mybir.dt.int32
U32 = mybir.dt.uint32
U16 = mybir.dt.uint16
U8 = mybir.dt.uint8
FP8X4 = mybir.dt.float8_e4m3fn_x4
FP4X4 = mybir.dt.float4_e2m1fn_x4
ALU = mybir.AluOpType
ACT = mybir.ActivationFunctionType
AXIS = mybir.AxisListType

P = 128
PACK = 4
QUADRANT = 32
LIST_ROWS = 16
GAIN = 512.0
HALF = SLOTS // 2
BASE_COLS = T // 2
STORE_COLS = 512


def tile_attend_hvdirect_twoside_s_kernel(
    tc, query, keys_words, keys_scales, averse, gout, vals_words, vals_scales, dquery, base, offs, out
):
    nc = tc.nc
    with ExitStack() as ctx:
        held = ctx.enter_context(tc.tile_pool(name="held", bufs=1))
        psum = ctx.enter_context(tc.psum_pool(name="psum", bufs=1))

        def sb(name, cols, dtype=F32, reuses=None):
            return held.tile([P, cols], dtype, name=name, tag=reuses or name, align_bytes=64)

        def pair(name, cols):
            return [sb(name + str(s), cols) for s in (0, 1)]


        def load_words(name, words):
            pool = sb(name, T, U16)
            nc.sync.dma_start(pool[:].bitcast(I32), words[0].bitcast(I32))
            return pool

        def load_plane(name, scales):
            plane = sb(name, T, U8)
            nc.vector.memset(plane[:].bitcast(I32), 0)
            for r in range(4):
                nc.sync.dma_start(plane[r:P:QUADRANT, :].bitcast(I32), scales[0, r:16:4, :].bitcast(I32))
            return plane

        def load_rows(name, rows):
            raw = held.tile([P, PACK, Q], F32, name=name, tag=name, align_bytes=64)
            nc.sync.dma_start(raw[:], rows.rearrange("(p j) q -> p j q", j=PACK))
            return raw

        offsets = held.tile([P, SLOTS // LIST_ROWS], U16, name="offsets")
        key_pool = load_words("key_pool", keys_words)
        nc.sync.dma_start(offsets[:], offs)
        key_pool_plane = load_plane("key_pool_plane", keys_scales)
        query_raw = load_rows("query_raw", query)
        val_pool = load_words("val_pool", vals_words)
        dquery_raw = load_rows("dquery_raw", dquery)
        gout_raw = load_rows("gout_raw", gout)
        val_pool_plane = load_plane("val_pool_plane", vals_scales)
        av = sb("av", 1)
        nc.sync.dma_start(av[:], averse)


        def gather(name, window, dtype, reuses=None):
            picked = sb(name, SLOTS, dtype, reuses)
            nc.vector.tensor_copy(picked[:], window[:].indirect(offsets[:]))
            return picked

        def quantize(name, raw):
            grouped = held.tile([P, Q, PACK], BF16, name=name + "_bf16", tag=name + "_bf16", align_bytes=64)
            nc.scalar.copy(
                grouped[:].rearrange("p (c i) j -> p c j i", i=4), raw[:].rearrange("p j (c i) -> p c j i", i=4)
            )
            words = sb(name + "_words", Q, U32)
            plane = sb(name + "_plane", Q, U8)
            nc.vector.quantize_mx(
                out=words[:].bitcast(FP8X4), scales=plane[:], in_=grouped[:].rearrange("p q j -> p (q j)")
            )
            return words, plane

        def product(name, rows, listed_words, listed_plane):
            acc = psum.tile([Q, SLOTS], F32, name=name)
            nc.tensor.matmul_mx(
                out=acc[:],
                lhsT=rows[0][:].bitcast(FP8X4),
                lhsT_scale=rows[1][:],
                rhs=listed_words[:].bitcast(FP4X4),
                rhs_scale=listed_plane[:],
                start=True,
                stop=True,
            )
            return acc

        key_words = gather("key_words", key_pool, U16)
        key_plane = gather("key_plane", key_pool_plane, U8)
        a = product("a", quantize("query", query_raw), key_words, key_plane)
        val_words = gather("val_words", val_pool, U16, reuses="query_bf16")
        ta = product("ta", quantize("dquery", dquery_raw), key_words, key_plane)

        neg_a, neg_max, low = sb("neg_a", SLOTS), sb("neg_max", 1), sb("low", 1)
        nc.vector.tensor_scalar(neg_a[:], a[:], -1.0, None, ALU.mult, ALU.min, accum_out=neg_max[:])
        nc.vector.tensor_reduce(low[:], a[:], AXIS.X, ALU.min)

        gout_mx = quantize("gout", gout_raw)
        val_plane = gather("val_plane", val_pool_plane, U8)
        c0 = product("c0", gout_mx, val_words, val_plane)

        p = (sb("p0", SLOTS, reuses="gout_raw"), sb("p1", SLOTS))
        total = pair("total", 1)
        nc.scalar.activation(p[0][:], neg_a[:], ACT.Exp, bias=neg_max[:], scale=-1.0, accum_out=total[0][:])
        ta_sb = sb("ta_sb", SLOTS, reuses="neg_max")
        nc.scalar.copy(ta_sb[:], ta[:])
        nc.scalar.activation(p[1][:], neg_a[:], ACT.Exp, bias=low[:], scale=1.0, accum_out=total[1][:])

        result = []
        for n, freed in enumerate(("key_pool", "val_pool")):
            result.append(sb("result" + str(n), BASE_COLS, reuses=freed))
            nc.sync.dma_start(result[n][:], base[:, n * BASE_COLS : (n + 1) * BASE_COLS])

        neg_inv, mean_t, mean_c, mean_c_inv, means_inv, cov, p_factor = (
            pair(name, 1) for name in ("neg_inv", "mean_t", "mean_c", "mean_c_inv", "means_inv", "cov", "p_factor")
        )
        rt = (sb("rt0", SLOTS), sb("rt1", SLOTS, reuses="val_pool_plane"))
        rc, centred = pair("rc", SLOTS), pair("centred", SLOTS)

        def times(dst, src, factor, accum_out=None):
            nc.scalar.activation(dst[:], src[:], ACT.Copy, scale=factor, accum_out=accum_out)

        stt = nc.vector.scalar_tensor_tensor

        inv = {}
        for s, freed in ((1, None), (0, "total1")):
            inv[s] = sb("inv" + str(s), 1, reuses=freed)
            nc.vector.reciprocal(inv[s][:], total[s][:])
            times(neg_inv[s], inv[s], -1.0)

        pt = sb("pt", SLOTS)
        nc.gpsimd.tensor_tensor(pt[:], p[0][:], ta_sb[:], ALU.mult)
        placed = sb("placed", T, reuses="neg_max")
        nc.gpsimd.memset(placed[:], 0.0)
        times(rt[0], pt, inv[0][:], accum_out=mean_t[0][:])
        stt(rt[1][:], ta[:], inv[1][:], p[1][:], ALU.mult, ALU.mult, accum_out=mean_t[1][:])

        for s in (0, 1):
            stt(rc[s][:], c0[:], inv[s][:], p[s][:], ALU.mult, ALU.mult, accum_out=mean_c[s][:])
            times(mean_c_inv[s], mean_c[s], inv[s][:])
            times(means_inv[s], mean_t[s], mean_c_inv[s][:])
        for s in (1, 0):
            stt(centred[s][:], ta[:], mean_t[s][:], rc[s][:], ALU.subtract, ALU.mult, accum_out=cov[s][:])
            nc.scalar.activation(p_factor[s][:], cov[s][:], ACT.Identity, bias=means_inv[s][:], scale=neg_inv[s][:])

        for h in range(SLOTS // HALF):
            cols = slice(h * HALF, (h + 1) * HALF)
            entries = offsets[:, h * HALF // LIST_ROWS : (h + 1) * HALF // LIST_ROWS]
            part = [sb("part%d%d" % (h, s), HALF, reuses="side0%d" % s if h else None) for s in (0, 1)]
            side = pair("side%d" % h, HALF)
            neg_tda = sb("neg_tda%d" % h, HALF)
            for s in (1, 0):
                stt(part[s][:], rt[s][:, cols], mean_c[s][:], centred[s][:, cols], ALU.mult, ALU.subtract)
            for s in (1, 0):
                stt(side[s][:], p[s][:, cols], p_factor[s][:], part[s][:], ALU.mult, ALU.subtract)
            stt(neg_tda[:], side[1][:], av[:], side[0][:], ALU.mult, ALU.subtract)
            nc.scalar.activation(placed[:].indirect(entries), neg_tda[:], ACT.Copy, scale=-GAIN)

        for n, first in enumerate(range(0, T, STORE_COLS)):
            cols = slice(first, first + STORE_COLS)
            piece = result[first // BASE_COLS][:, first % BASE_COLS : first % BASE_COLS + STORE_COLS]
            nc.vector.tensor_tensor(piece, piece, placed[:, cols], ALU.add)
            (nc.sync, nc.scalar)[n % 2].dma_start(out[:, cols], piece)
